import numpy as np
import ml_dtypes


def mxq(x, axis, fmt="e4m3"):
    dtype, down = {"e4m3": (ml_dtypes.float8_e4m3fn, 7), "e5m2": (ml_dtypes.float8_e5m2, 14)}[fmt]
    v = np.moveaxis(np.asarray(x, np.float32).astype(ml_dtypes.bfloat16).astype(np.float64), axis, -1)
    blocks = v.reshape(v.shape[:-1] + (-1, 32))
    amax = np.abs(blocks).max(-1, keepdims=True)
    byte = np.maximum(np.where(amax > 0, np.frexp(amax)[1] - 1 + 127, 0) - down, 1)
    scale = np.exp2(byte - 127.0)
    codes = (blocks / scale).astype(np.float32).astype(dtype).astype(np.float64)
    return np.moveaxis((codes * scale).reshape(v.shape), -1, axis)


WIDE = False


def mx_kscale(k):
    if not WIDE:
        return np.ones(k)
    levels = np.array([10, -10, 5, -5, 0])
    if k % 512:
        return np.exp2(np.random.permutation(np.resize(levels, k // 32))).repeat(32)
    a = np.empty((k // 512, 16))
    for p in range(k // 512):
        a[p, :8] = np.random.permutation(np.resize(levels, 8))
        for g in range(8):
            far = levels[np.abs(levels - a[p, g]) >= 10]
            a[p, g + 8] = far[np.random.randint(len(far))]
    return np.exp2(a.ravel()).repeat(32)


def f64(x):
    return np.asarray(x).astype(np.float64)


def striped(idx):
    return np.tile(idx.reshape(-1, 16).T, (8, 1)).astype(np.uint16)


def unstriped(offs):
    return offs[:16].T.reshape(-1).astype(np.int64)


def striped8(idx):
    return np.concatenate([x.reshape(-1, 16).T for x in idx]).astype(np.uint16)


def runs(offs, k):
    lists = np.stack([offs[16 * r : 16 * r + 16].T.reshape(-1) for r in range(8)]).astype(np.int64)
    return lists[np.arange(k) % 512 // 64]


def pack_weight(w):
    k, n = w.shape
    w = f64(np.asarray(w, np.float32).astype(ml_dtypes.bfloat16)).reshape(k // 32, 32, n)
    amax = np.abs(w).max(1)
    byte = np.clip(np.where(amax > 0, np.frexp(amax)[1] - 1 + 127 - 7, 1), 1, 254)
    scaled = (w * np.exp2(127.0 - byte)[:, None, :]).reshape(k, n).astype(np.float32)
    words = np.ascontiguousarray(scaled.reshape(k // 512, 128, 4, n).transpose(0, 1, 3, 2)).astype(ml_dtypes.float8_e4m3fn).view(np.uint8)
    return words, np.ascontiguousarray(byte.astype(np.uint8).reshape(k // 512, 16, n))


def unpack_weight(words, scales):
    g, p, n, _ = words.shape
    vals = np.ascontiguousarray(words).view(ml_dtypes.float8_e4m3fn).astype(np.float64) * np.repeat(np.exp2(scales.astype(np.float64) - 127.0), 8, axis=1)[..., None]
    return vals.transpose(0, 1, 3, 2).reshape(g * 512, n)


K, T, S, H, C = 512, 2048, 512, 512, 512


def setup_inputs():
    n = np.random.standard_normal
    s = mx_kscale(K)[:, None]
    packed_xT = pack_weight(n((K, T)) * s)
    return {
        "x_words": packed_xT[0],
        "x_scales": packed_xT[1],
        "w1": (n((K, H)) / np.sqrt(K) / s).astype(np.float32),
        "gs": (np.random.uniform(0.5, 1.5, (K, 1)) / s).astype(np.float32),
        "wb": (n((K, S)) / np.sqrt(K) / s).astype(np.float32),
        "offs": striped(np.random.permutation(T)[:S]),
        "n1": striped8(np.stack([np.random.permutation(S) for _ in range(8)])),
        "n2": striped8(np.stack([np.random.permutation(S) for _ in range(8)])),
        "cand": striped(np.random.permutation(T)[:C]),
        "cb": striped(np.random.permutation(T)[:C]),
        "n3": striped8(np.stack([np.random.permutation(S) for _ in range(8)])),
        "n4": striped8(np.stack([np.random.permutation(S) for _ in range(8)])),
        "n5": striped8(np.stack([np.random.permutation(S) for _ in range(8)])),
    }


def reference(x_words, x_scales, w1, gs, wb, offs, n1, n2, cand, cb, n3, n4, n5):
    x_cand = unpack_weight(x_words, x_scales)[:, unstriped(cand)]
    xq = unpack_weight(x_words, x_scales)[:, unstriped(offs)]
    y = mxq(f64(w1), 0, "e4m3").T @ xq
    z = f64(gs) * (0.75 * ((y - (y[np.arange(H)[:, None], runs(n1, H)])) * (y - (y[np.arange(H)[:, None], runs(n2, H)]))))
    a = 0.0625 * ((x_cand.T @ mxq(z, 0, "e4m3")))
    x_cb = unpack_weight(x_words, x_scales)[:, unstriped(cb)]
    b = x_cb.T @ mxq(f64(wb), 0, "e4m3")
    return np.maximum(np.minimum(a - (0.5 * (a[np.arange(C)[:, None], runs(n3, C)])), b[np.arange(C)[:, None], runs(n4, C)]), b[np.arange(C)[:, None], runs(n5, C)])

@@ -1,0 +1,204 @@
+from contextlib import ExitStack
+
+import concourse.mybir as mybir
+
+K, T, S, H, C = 512, 2048, 512, 512, 512
+FLOPS = 2 * K * H * S + 2 * K * C * S + 2 * K * C * S
+
+F32 = mybir.dt.float32
+BF16 = mybir.dt.bfloat16
+I32 = mybir.dt.int32
+U32 = mybir.dt.uint32
+U16 = mybir.dt.uint16
+U8 = mybir.dt.uint8
+FP8X4 = mybir.dt.float8_e4m3fn_x4
+COPY = mybir.ActivationFunctionType.Copy
+ALU = mybir.AluOpType
+
+P = 128
+PACK = 4
+HALF = 256
+LIST_COLS = S // 16
+
+
+def tile_picked_cdswclampbquad_none_p_kernel(tc, x_words, x_scales, w1, gs, wb, offs, n1, n2, cand, cb, n3, n4, n5, out):
+    nc = tc.nc
+    with ExitStack() as ctx:
+        lists = ctx.enter_context(tc.tile_pool(name="lists", bufs=1))
+        keep = ctx.enter_context(tc.tile_pool(name="keep", bufs=1))
+        ring = ctx.enter_context(tc.tile_pool(name="ring", bufs=3))
+        psum = ctx.enter_context(tc.psum_pool(name="psum", bufs=1))
+
+        def load_list(name, src):
+            t = lists.tile([P, LIST_COLS], U16, name=name)
+            nc.sync.dma_start(t[:], src)
+            return t
+
+        def half_of(lst, h):
+            return lst[:, h * (HALF // 16) : (h + 1) * (HALF // 16)]
+
+        def cols(h):
+            return slice(h * HALF, (h + 1) * HALF)
+
+        xs = keep.tile([P, T], U8, name="xs", align_bytes=64)
+        nc.vector.memset(xs[:].bitcast(I32), 0)
+        offs_l = load_list("offs_l", offs)
+        cand_l = load_list("cand_l", cand)
+        cb_l = load_list("cb_l", cb)
+        for q in range(4):
+            nc.sync.dma_start(xs[32 * q : 32 * q + 4, :].bitcast(I32), x_scales[0, 4 * q : 4 * q + 4, :].bitcast(I32))
+        xw = keep.tile([P, T], U32, name="xw", align_bytes=64)
+        nc.sync.dma_start(xw[:].bitcast(I32), x_words[0].rearrange("p n t -> p (n t)").bitcast(I32))
+        w1_raw, wb_raw = [], []
+        for name, w, raws in (("w1_raw", w1, w1_raw), ("wb_raw", wb, wb_raw)):
+            for h in range(2):
+                raw = keep.tile([P, PACK, HALF], F32, name="%s%d" % (name, h), tag="%s%d" % (name, h), align_bytes=64)
+                nc.sync.dma_start(raw[:], w.rearrange("(p j) c -> p j c", j=PACK)[:, :, cols(h)])
+                raws.append(raw)
+        gs_t = keep.tile([P, PACK], F32, name="gs_t")
+        nc.sync.dma_start(gs_t[:], gs.rearrange("(p t) o -> p (t o)", t=PACK))
+        n1_l = load_list("n1_l", n1)
+        n2_l = load_list("n2_l", n2)
+        n4_l = load_list("n4_l", n4)
+        n5_l = load_list("n5_l", n5)
+        n3_l = load_list("n3_l", n3)
+
+        def gather_scales(name, lst):
+            g = keep.tile([P, S], U8, name=name, align_bytes=64)
+            nc.vector.tensor_copy(g[:], xs[:].indirect(lst[:]))
+            return g
+
+        def deal_scales(name, g):
+            d = keep.tile([P, S], U8, name=name, align_bytes=64)
+            nc.vector.tensor_copy(d[:].rearrange("p (t m) -> p t m", t=PACK), g[:].rearrange("p (m t) -> p t m", t=PACK))
+            return d
+
+        def gather_words_dealt(name, lst, tag):
+            d = keep.tile([P, S], U32, name=name, tag=tag, align_bytes=64)
+            nc.vector.tensor_copy(d[:].rearrange("p (t m) -> p m t", t=PACK), xw[:].indirect(lst[:]))
+            return d
+
+        xq_s = gather_scales("xq_s", offs_l)
+        cb_g = gather_scales("cb_g", cb_l)
+        cand_g = gather_scales("cand_g", cand_l)
+        cb_s = deal_scales("cb_s", cb_g)
+        cand_s = deal_scales("cand_s", cand_g)
+        xq_w = keep.tile([P, S], U32, name="xq_w", align_bytes=64)
+        nc.vector.tensor_copy(xq_w[:], xw[:].indirect(offs_l[:]))
+
+        w1_bf = keep.tile([P, H * PACK], BF16, name="w1_bf", tag="w1_bf", align_bytes=64)
+        for h in range(2):
+            m = slice(h * (HALF // PACK), (h + 1) * (HALF // PACK))
+            nc.scalar.activation(
+                w1_bf[:].rearrange("p (t m j) -> p m t j", t=PACK, j=PACK)[:, m],
+                w1_raw[h][:].rearrange("p j (m t) -> p m t j", t=PACK),
+                COPY,
+            )
+        gain = keep.tile([P, PACK], F32, name="gain")
+        nc.scalar.activation(gain[:], gs_t[:], COPY, scale=0.75)
+
+        def quantize(name, src, width):
+            w = keep.tile([P, width], U32, name=name + "_w", align_bytes=64)
+            s = keep.tile([P, width], U8, name=name + "_s", align_bytes=64)
+            nc.vector.quantize_mx(out=w[:].bitcast(FP8X4), scales=s[:], in_=src)
+            return w, s
+
+        w1_w, w1_s = quantize("w1q", w1_bf[:], H)
+
+        def product(acc, lw, ls, t, rw, rs):
+            m = slice(t * P, (t + 1) * P)
+            nc.tensor.matmul_mx(out=acc, lhsT=lw[:, m].bitcast(FP8X4), lhsT_scale=ls[:, m],
+                                rhs=rw[:].bitcast(FP8X4), rhs_scale=rs[:], start=True, stop=True)
+
+        y_win, y_cpy = [], []
+        for t in range(PACK):
+            acc = psum.tile([P, S], F32, name="y_ps%d" % t, tag="ya%d" % t)
+            product(acc[:], w1_w, w1_s, t, xq_w, xq_s)
+            win = keep.tile([P, S], F32, name="y_win%d" % t)
+            cpy = keep.tile([P, S], F32, name="y_cpy%d" % t)
+            nc.scalar.copy(win[:], acc[:])
+            nc.scalar.copy(cpy[:], acc[:])
+            y_win.append(win)
+            y_cpy.append(cpy)
+
+        cb_w = gather_words_dealt("cb_w", cb_l, "cb_w")
+        cand_w = gather_words_dealt("cand_w", cand_l, "w1_bf")
+
+        wb_bf = keep.tile([P, S * PACK], BF16, name="wb_bf", align_bytes=64)
+        for h in range(2):
+            nc.vector.tensor_copy(
+                wb_bf[:, h * HALF * PACK : (h + 1) * HALF * PACK].rearrange("p (c i j) -> p c j i", i=4, j=PACK),
+                wb_raw[h][:].rearrange("p j (c i) -> p c j i", i=4),
+            )
+        wb_w, wb_s = quantize("wbq", wb_bf[:], S)
+        g4, g5 = [], []
+        for t in range(PACK):
+            acc = psum.tile([P, S], F32, name="b_ps%d" % t, tag="b%d" % t)
+            product(acc[:], cb_w, cb_s, t, wb_w, wb_s)
+            win = keep.tile([P, S], F32, name="b_win%d" % t)
+            nc.scalar.copy(win[:], acc[:])
+            for name, lst, dst in (("g4", n4_l, g4), ("g5", n5_l, g5)):
+                g = keep.tile([P, S], F32, name="%s_%d" % (name, t))
+                for h in range(2):
+                    nc.scalar.activation(g[:, cols(h)], win[:].indirect(half_of(lst, h)), COPY)
+                dst.append(g)
+
+        a_ps = [psum.tile([P, S], F32, name="a_ps%d" % t, tag="ya%d" % t) for t in range(PACK)]
+        a_win = [keep.tile([P, S], F32, name="a_win%d" % t) for t in range(PACK)]
+        planes = [keep.tile([P, PACK, HALF], BF16, name="z_planes%d" % h, align_bytes=64) for h in range(2)]
+        z_bf = [keep.tile([P, HALF * PACK], BF16, name="z_bf%d" % h, align_bytes=64) for h in range(2)]
+
+        def diff(lst, h, t, tag):
+            d = ring.tile([P, HALF], F32, name=tag, tag=tag)
+            nc.vector.tensor_tensor(d[:], y_win[t][:].indirect(half_of(lst, h)), y_cpy[t][:, cols(h)], ALU.subtract)
+            return d
+
+        def z_plane(h, t, d1, d2):
+            nc.vector.scalar_tensor_tensor(planes[h][:, t, :], d1[:], gain[:, t : t + 1], d2[:], ALU.mult, ALU.mult)
+
+        def z_weave(h):
+            nc.vector.tensor_copy(z_bf[h][:].rearrange("p (c i t) -> p c t i", i=4, t=PACK), planes[h][:].rearrange("p t (c i) -> p c t i", i=4))
+
+        def score(h):
+            z_w, z_s = quantize("zq%d" % h, z_bf[h][:], HALF)
+            for t in range(PACK):
+                product(a_ps[t][:, cols(h)], cand_w, cand_s, t, z_w, z_s)
+                nc.scalar.activation(a_win[t][:, cols(h)], a_ps[t][:, cols(h)], COPY, scale=0.0625)
+
+        pending = None
+        for h in range(2):
+            for t in range(PACK):
+                d1 = diff(n1_l, h, t, "d1")
+                if pending is not None:
+                    z_plane(*pending)
+                d2 = diff(n2_l, h, t, "d2")
+                pending = (h, t, d1, d2)
+                if h == 1 and t == 0:
+                    z_weave(0)
+                if h == 1 and t == 1:
+                    score(0)
+        z_plane(*pending)
+        z_weave(1)
+        score(1)
+
+        out_rows = out.rearrange("(p t) n -> p t n", t=PACK)
+        units = [(t, h) for t in range(PACK) for h in range(2)]
+        us, vs = {}, {}
+        for step in range(len(units) + 2):
+            if step < len(units):
+                t, h = units[step]
+                g3 = ring.tile([P, HALF], F32, name="g3", tag="g3")
+                nc.scalar.activation(g3[:], a_win[t][:].indirect(half_of(n3_l, h)), COPY)
+                u = ring.tile([P, HALF], F32, name="u", tag="u")
+                nc.vector.scalar_tensor_tensor(u[:], g3[:], -0.5, a_win[t][:, cols(h)], ALU.mult, ALU.add)
+                us[step] = u
+            if 0 <= step - 1 < len(units):
+                t, h = units[step - 1]
+                v = ring.tile([P, HALF], F32, name="v", tag="v")
+                nc.vector.tensor_tensor(v[:], us[step - 1][:], g4[t][:, cols(h)], ALU.min)
+                vs[step - 1] = v
+            if 0 <= step - 2:
+                t, h = units[step - 2]
+                o = keep.tile([P, HALF], F32, name="o%d" % (step - 2))
+                nc.vector.tensor_tensor(o[:], vs[step - 2][:], g5[t][:, cols(h)], ALU.max)
+                nc.sync.dma_start(out_rows[:, t, cols(h)], o[:])

@@ -42,19 +42,22 @@ def tile_picked_cdswclampbquad_none_p_kernel(tc, x_words, x_scales, w1, gs, wb, 
 
         xs = keep.tile([P, T], U8, name="xs", align_bytes=64)
         nc.vector.memset(xs[:].bitcast(I32), 0)
+        def load_half(name, w, h):
+            raw = keep.tile([P, PACK, HALF], F32, name="%s%d" % (name, h), tag="%s%d" % (name, h), align_bytes=64)
+            nc.sync.dma_start(raw[:], w.rearrange("(p j) c -> p j c", j=PACK)[:, :, cols(h)])
+            return raw
+
+        xw = keep.tile([P, T], U32, name="xw", align_bytes=64)
+        x_rows = x_words[0].rearrange("p n t -> p (n t)").bitcast(I32)
         offs_l = load_list("offs_l", offs)
-        cand_l = load_list("cand_l", cand)
-        cb_l = load_list("cb_l", cb)
+        nc.sync.dma_start(xw[:, : T // 2].bitcast(I32), x_rows[:, : T // 2])
         for q in range(4):
             nc.sync.dma_start(xs[32 * q : 32 * q + 4, :].bitcast(I32), x_scales[0, 4 * q : 4 * q + 4, :].bitcast(I32))
-        xw = keep.tile([P, T], U32, name="xw", align_bytes=64)
-        nc.sync.dma_start(xw[:].bitcast(I32), x_words[0].rearrange("p n t -> p (n t)").bitcast(I32))
-        w1_raw, wb_raw = [], []
-        for name, w, raws in (("w1_raw", w1, w1_raw), ("wb_raw", wb, wb_raw)):
-            for h in range(2):
-                raw = keep.tile([P, PACK, HALF], F32, name="%s%d" % (name, h), tag="%s%d" % (name, h), align_bytes=64)
-                nc.sync.dma_start(raw[:], w.rearrange("(p j) c -> p j c", j=PACK)[:, :, cols(h)])
-                raws.append(raw)
+        cb_l = load_list("cb_l", cb)
+        nc.sync.dma_start(xw[:, T // 2 :].bitcast(I32), x_rows[:, T // 2 :])
+        w1_raw = [load_half("w1_raw", w1, h) for h in range(2)]
+        cand_l = load_list("cand_l", cand)
+        wb_raw = [load_half("wb_raw", wb, h) for h in range(2)]
         gs_t = keep.tile([P, PACK], F32, name="gs_t")
         nc.sync.dma_start(gs_t[:], gs.rearrange("(p t) o -> p (t o)", t=PACK))
         n1_l = load_list("n1_l", n1)
@@ -63,8 +66,8 @@ def tile_picked_cdswclampbquad_none_p_kernel(tc, x_words, x_scales, w1, gs, wb, 
         n5_l = load_list("n5_l", n5)
         n3_l = load_list("n3_l", n3)
 
-        def gather_scales(name, lst):
-            g = keep.tile([P, S], U8, name=name, align_bytes=64)
+        def gather_scales(name, lst, tag):
+            g = keep.tile([P, S], U8, name=name, tag=tag, align_bytes=64)
             nc.vector.tensor_copy(g[:], xs[:].indirect(lst[:]))
             return g
 
@@ -78,13 +81,11 @@ def tile_picked_cdswclampbquad_none_p_kernel(tc, x_words, x_scales, w1, gs, wb, 
             nc.vector.tensor_copy(d[:].rearrange("p (t m) -> p m t", t=PACK), xw[:].indirect(lst[:]))
             return d
 
-        xq_s = gather_scales("xq_s", offs_l)
-        cb_g = gather_scales("cb_g", cb_l)
-        cand_g = gather_scales("cand_g", cand_l)
-        cb_s = deal_scales("cb_s", cb_g)
-        cand_s = deal_scales("cand_s", cand_g)
-        xq_w = keep.tile([P, S], U32, name="xq_w", align_bytes=64)
+        xq_s = gather_scales("xq_s", offs_l, "xq_s")
+        xq_w = keep.tile([P, S], U32, name="xq_w", tag="xq_w", align_bytes=64)
         nc.vector.tensor_copy(xq_w[:], xw[:].indirect(offs_l[:]))
+        cb_g = gather_scales("cb_g", cb_l, "cb_g")
+        cb_s = deal_scales("cb_s", cb_g)
 
         w1_bf = keep.tile([P, H * PACK], BF16, name="w1_bf", tag="w1_bf", align_bytes=64)
         for h in range(2):
@@ -110,95 +111,118 @@ def tile_picked_cdswclampbquad_none_p_kernel(tc, x_words, x_scales, w1, gs, wb, 
             nc.tensor.matmul_mx(out=acc, lhsT=lw[:, m].bitcast(FP8X4), lhsT_scale=ls[:, m],
                                 rhs=rw[:].bitcast(FP8X4), rhs_scale=rs[:], start=True, stop=True)
 
-        y_win, y_cpy = [], []
+        wb_bf = keep.tile([P, S * PACK], BF16, name="wb_bf", tag="wb_bf", align_bytes=64)
+        for h in range(2):
+            nc.scalar.activation(
+                wb_bf[:, h * HALF * PACK : (h + 1) * HALF * PACK].rearrange("p (c i j) -> p c j i", i=4, j=PACK),
+                wb_raw[h][:].rearrange("p j (c i) -> p c j i", i=4),
+                COPY,
+            )
+
+        last = PACK - 1
+        y_win = [keep.tile([P, S], F32, name="y_win0")]
+        y_win = y_win + [keep.tile([P, 2 * S], F32, name="y_win%d" % t) for t in range(1, last)]
+        y_win += [keep.tile([P, S], F32, name="y_win3", tag="wb_raw1", align_bytes=64)]
+        y_cpy = [y_win[t + 1][:, S:] for t in range(last - 1)]
+        y_cpy += [keep.tile([P, S], F32, name="y_cpy2")[:]]
         for t in range(PACK):
             acc = psum.tile([P, S], F32, name="y_ps%d" % t, tag="ya%d" % t)
             product(acc[:], w1_w, w1_s, t, xq_w, xq_s)
-            win = keep.tile([P, S], F32, name="y_win%d" % t)
-            cpy = keep.tile([P, S], F32, name="y_cpy%d" % t)
-            nc.scalar.copy(win[:], acc[:])
-            nc.scalar.copy(cpy[:], acc[:])
-            y_win.append(win)
-            y_cpy.append(cpy)
+            nc.scalar.copy(y_win[t][:, :S], acc[:])
+            if t < last:
+                nc.sync.dma_start(y_cpy[t], y_win[t][:, :S])
+        y_g = []
+        for i, lst in enumerate((n1_l, n2_l)):
+            g = keep.tile([P, S], F32, name="y_g%d" % i)
+            for h in range(2):
+                nc.scalar.activation(g[:, cols(h)], y_win[last][:].indirect(half_of(lst, h)), COPY)
+            y_g.append(g)
 
-        cb_w = gather_words_dealt("cb_w", cb_l, "cb_w")
-        cand_w = gather_words_dealt("cand_w", cand_l, "w1_bf")
+        cb_w = gather_words_dealt("cb_w", cb_l, "w1_bf")
+        cand_g = gather_scales("cand_g", cand_l, "w1_raw1")
+        cand_s = deal_scales("cand_s", cand_g)
+        cand_w = gather_words_dealt("cand_w", cand_l, "w1_raw1")
 
-        wb_bf = keep.tile([P, S * PACK], BF16, name="wb_bf", align_bytes=64)
-        for h in range(2):
-            nc.vector.tensor_copy(
-                wb_bf[:, h * HALF * PACK : (h + 1) * HALF * PACK].rearrange("p (c i j) -> p c j i", i=4, j=PACK),
-                wb_raw[h][:].rearrange("p j (c i) -> p c j i", i=4),
-            )
         wb_w, wb_s = quantize("wbq", wb_bf[:], S)
-        g4, g5 = [], []
+        b_g, b_win = {}, []
         for t in range(PACK):
             acc = psum.tile([P, S], F32, name="b_ps%d" % t, tag="b%d" % t)
             product(acc[:], cb_w, cb_s, t, wb_w, wb_s)
             win = keep.tile([P, S], F32, name="b_win%d" % t)
             nc.scalar.copy(win[:], acc[:])
-            for name, lst, dst in (("g4", n4_l, g4), ("g5", n5_l, g5)):
-                g = keep.tile([P, S], F32, name="%s_%d" % (name, t))
+            b_win.append(win)
+            for i, lst in enumerate((n4_l, n5_l)):
                 for h in range(2):
-                    nc.scalar.activation(g[:, cols(h)], win[:].indirect(half_of(lst, h)), COPY)
-                dst.append(g)
+                    if t < last or (i, h) == (0, 0):
+                        g = keep.tile([P, HALF], F32, name="b_g%d%d%d" % (i, t, h))
+                        nc.scalar.activation(g[:], win[:].indirect(half_of(lst, h)), COPY)
+                        b_g[i, t, h] = g[:]
 
         a_ps = [psum.tile([P, S], F32, name="a_ps%d" % t, tag="ya%d" % t) for t in range(PACK)]
         a_win = [keep.tile([P, S], F32, name="a_win%d" % t) for t in range(PACK)]
-        planes = [keep.tile([P, PACK, HALF], BF16, name="z_planes%d" % h, align_bytes=64) for h in range(2)]
-        z_bf = [keep.tile([P, HALF * PACK], BF16, name="z_bf%d" % h, align_bytes=64) for h in range(2)]
+        planes = keep.tile([P, PACK, S], BF16, name="z_planes", align_bytes=64)
+        z_bf = [keep.tile([P, HALF * PACK], BF16, name="z_bf%d" % h, tag="z_bf%d" % h, align_bytes=64) for h in range(2)]
 
-        def diff(lst, h, t, tag):
-            d = ring.tile([P, HALF], F32, name=tag, tag=tag)
-            nc.vector.tensor_tensor(d[:], y_win[t][:].indirect(half_of(lst, h)), y_cpy[t][:, cols(h)], ALU.subtract)
-            return d
+        def diff(d, i, t):
+            lst = (n1_l, n2_l)[i]
+            if t == 0:
+                for h in range(2):
+                    nc.vector.tensor_tensor(d[:, i * S + h * HALF : i * S + (h + 1) * HALF], y_win[t][:].indirect(half_of(lst, h)), y_cpy[t][:, cols(h)], ALU.subtract)
+            elif t < last:
+                nc.vector.tensor_tensor(d[:, i * S : (i + 1) * S], y_win[t][:].indirect(lst[:]), y_cpy[t], ALU.subtract)
+            else:
+                nc.vector.tensor_tensor(d[:, i * S : (i + 1) * S], y_g[i][:], y_win[t][:, :S], ALU.subtract)
 
-        def z_plane(h, t, d1, d2):
-            nc.vector.scalar_tensor_tensor(planes[h][:, t, :], d1[:], gain[:, t : t + 1], d2[:], ALU.mult, ALU.mult)
+        def z_plane(t, d, lo, hi):
+            nc.vector.scalar_tensor_tensor(planes[:, t, lo:hi], d[:, lo:hi], gain[:, t : t + 1], d[:, S + lo : S + hi], ALU.mult, ALU.mult)
 
-        def z_weave(h):
-            nc.vector.tensor_copy(z_bf[h][:].rearrange("p (c i t) -> p c t i", i=4, t=PACK), planes[h][:].rearrange("p t (c i) -> p c t i", i=4))
-
-        def score(h):
-            z_w, z_s = quantize("zq%d" % h, z_bf[h][:], HALF)
-            for t in range(PACK):
-                product(a_ps[t][:, cols(h)], cand_w, cand_s, t, z_w, z_s)
-                nc.scalar.activation(a_win[t][:, cols(h)], a_ps[t][:, cols(h)], COPY, scale=0.0625)
-
-        pending = None
+        prev = None
+        for t in range(PACK):
+            d = keep.tile([P, 2 * S], F32, name="d%d" % t, tag=("wb_bf", "w1_bf")[t % 2], align_bytes=64)
+            diff(d, 0, t)
+            if prev is not None:
+                z_plane(t - 1, prev, 0, S)
+            diff(d, 1, t)
+            prev = d
         for h in range(2):
-            for t in range(PACK):
-                d1 = diff(n1_l, h, t, "d1")
-                if pending is not None:
-                    z_plane(*pending)
-                d2 = diff(n2_l, h, t, "d2")
-                pending = (h, t, d1, d2)
-                if h == 1 and t == 0:
-                    z_weave(0)
-                if h == 1 and t == 1:
-                    score(0)
-        z_plane(*pending)
-        z_weave(1)
-        score(1)
+            z_plane(last, prev, h * HALF, (h + 1) * HALF)
+        for h in range(2):
+            nc.vector.tensor_copy(z_bf[h][:].rearrange("p (c i t) -> p c t i", i=4, t=PACK), planes[:, :, cols(h)].rearrange("p t (c i) -> p c t i", i=4))
+        zq = [quantize("zq%d" % h, z_bf[h][:], HALF) for h in range(2)]
+        for t in range(PACK):
+            for h in range(2):
+                product(a_ps[t][:, cols(h)], cand_w, cand_s, t, *zq[h])
+        g = keep.tile([P, HALF], F32, name="g4_last", tag="z_bf0", align_bytes=64)
+        nc.vector.tensor_copy(g[:], b_win[last][:].indirect(half_of(n4_l, 1)))
+        b_g[0, last, 1] = g[:]
+        g = keep.tile([P, S], F32, name="g5_last", tag="z_bf1", align_bytes=64)
+        for h in range(2):
+            nc.vector.tensor_copy(g[:, cols(h)], b_win[last][:].indirect(half_of(n5_l, h)))
+            b_g[1, last, h] = g[:, cols(h)]
 
         out_rows = out.rearrange("(p t) n -> p t n", t=PACK)
-        units = [(t, h) for t in range(PACK) for h in range(2)]
-        us, vs = {}, {}
-        for step in range(len(units) + 2):
-            if step < len(units):
-                t, h = units[step]
-                g3 = ring.tile([P, HALF], F32, name="g3", tag="g3")
-                nc.scalar.activation(g3[:], a_win[t][:].indirect(half_of(n3_l, h)), COPY)
-                u = ring.tile([P, HALF], F32, name="u", tag="u")
-                nc.vector.scalar_tensor_tensor(u[:], g3[:], -0.5, a_win[t][:, cols(h)], ALU.mult, ALU.add)
-                us[step] = u
-            if 0 <= step - 1 < len(units):
-                t, h = units[step - 1]
-                v = ring.tile([P, HALF], F32, name="v", tag="v")
-                nc.vector.tensor_tensor(v[:], us[step - 1][:], g4[t][:, cols(h)], ALU.min)
-                vs[step - 1] = v
-            if 0 <= step - 2:
-                t, h = units[step - 2]
-                o = keep.tile([P, HALF], F32, name="o%d" % (step - 2))
-                nc.vector.tensor_tensor(o[:], vs[step - 2][:], g5[t][:, cols(h)], ALU.max)
-                nc.sync.dma_start(out_rows[:, t, cols(h)], o[:])
+        units = [(t, h * HALF, HALF) for t in range(PACK) for h in range(2)]
+        units = units[:-1] + [(last, HALF, HALF // 2), (last, HALF + HALF // 2, HALF // 2)]
+
+        def looked_up(i, t, lo, n):
+            return b_g[i, t, lo // HALF][:, lo % HALF : lo % HALF + n]
+
+        def finish(t, lo, n, v):
+            o = keep.tile([P, n], F32, name="o%d_%d" % (t, lo))
+            nc.vector.tensor_tensor(o[:], v[:, :n], looked_up(1, t, lo, n), ALU.max)
+            nc.sync.dma_start(out_rows[:, t, lo : lo + n], o[:])
+
+        waiting = None
+        for t, lo, n in units:
+            if lo == 0:
+                nc.scalar.activation(a_win[t][:], a_ps[t][:], COPY, scale=0.0625)
+            g3 = ring.tile([P, HALF], F32, name="g3", tag="g3")
+            nc.scalar.activation(g3[:, :n], a_win[t][:].indirect(n3_l[:, lo // 16 : (lo + n) // 16]), COPY)
+            u = ring.tile([P, HALF], F32, name="u", tag="u")
+            nc.vector.scalar_tensor_tensor(u[:, :n], g3[:, :n], -0.5, a_win[t][:, lo : lo + n], ALU.mult, ALU.add)
+            if waiting is not None:
+                finish(*waiting)
+            v = ring.tile([P, HALF], F32, name="v", tag="v")
+            nc.vector.tensor_tensor(v[:, :n], u[:, :n], looked_up(0, t, lo, n), ALU.min)
+            waiting = (t, lo, n, v)
+        finish(*waiting)

@@ -51,8 +51,8 @@ def tile_picked_cdswclampbquad_none_p_kernel(tc, x_words, x_scales, w1, gs, wb, 
         x_rows = x_words[0].rearrange("p n t -> p (n t)").bitcast(I32)
         offs_l = load_list("offs_l", offs)
         nc.sync.dma_start(xw[:, : T // 2].bitcast(I32), x_rows[:, : T // 2])
-        for q in range(4):
-            nc.sync.dma_start(xs[32 * q : 32 * q + 4, :].bitcast(I32), x_scales[0, 4 * q : 4 * q + 4, :].bitcast(I32))
+        for r in range(4):
+            nc.sync.dma_start(xs[r:P:32, :].bitcast(I32), x_scales[0, r:16:4, :].bitcast(I32))
         cb_l = load_list("cb_l", cb)
         nc.sync.dma_start(xw[:, T // 2 :].bitcast(I32), x_rows[:, T // 2 :])
         w1_raw = [load_half("w1_raw", w1, h) for h in range(2)]
@@ -73,19 +73,20 @@ def tile_picked_cdswclampbquad_none_p_kernel(tc, x_words, x_scales, w1, gs, wb, 
 
         def deal_scales(name, g):
             d = keep.tile([P, S], U8, name=name, align_bytes=64)
-            nc.vector.tensor_copy(d[:].rearrange("p (t m) -> p t m", t=PACK), g[:].rearrange("p (m t) -> p t m", t=PACK))
+            nc.vector.tensor_copy(d[:].bitcast(I32).rearrange("p (t g w) -> p t g w", t=PACK, g=8), g[:].bitcast(I32).rearrange("p (g t w) -> p t g w", t=PACK, g=8))
             return d
 
         def gather_words_dealt(name, lst, tag):
             d = keep.tile([P, S], U32, name=name, tag=tag, align_bytes=64)
-            nc.vector.tensor_copy(d[:].rearrange("p (t m) -> p m t", t=PACK), xw[:].indirect(lst[:]))
+            nc.vector.tensor_copy(d[:].rearrange("p (t g r) -> p g t r", t=PACK, g=8), xw[:].indirect(lst[:]))
             return d
 
         xq_s = gather_scales("xq_s", offs_l, "xq_s")
-        xq_w = keep.tile([P, S], U32, name="xq_w", tag="xq_w", align_bytes=64)
-        nc.vector.tensor_copy(xq_w[:], xw[:].indirect(offs_l[:]))
         cb_g = gather_scales("cb_g", cb_l, "cb_g")
         cb_s = deal_scales("cb_s", cb_g)
+        xq_w = keep.tile([P, S], U32, name="xq_w", tag="xq_w", align_bytes=64)
+        nc.vector.tensor_copy(xq_w[:], xw[:].indirect(offs_l[:]))
+        cb_w = gather_words_dealt("cb_w", cb_l, "cb_w")
 
         w1_bf = keep.tile([P, H * PACK], BF16, name="w1_bf", tag="w1_bf", align_bytes=64)
         for h in range(2):
@@ -112,38 +113,35 @@ def tile_picked_cdswclampbquad_none_p_kernel(tc, x_words, x_scales, w1, gs, wb, 
                                 rhs=rw[:].bitcast(FP8X4), rhs_scale=rs[:], start=True, stop=True)
 
         wb_bf = keep.tile([P, S * PACK], BF16, name="wb_bf", tag="wb_bf", align_bytes=64)
-        for h in range(2):
-            nc.scalar.activation(
+
+        def wb_views(h):
+            return (
                 wb_bf[:, h * HALF * PACK : (h + 1) * HALF * PACK].rearrange("p (c i j) -> p c j i", i=4, j=PACK),
                 wb_raw[h][:].rearrange("p j (c i) -> p c j i", i=4),
-                COPY,
             )
 
+        nc.scalar.activation(*wb_views(0), COPY)
+
         last = PACK - 1
-        y_win = [keep.tile([P, S], F32, name="y_win0")]
-        y_win = y_win + [keep.tile([P, 2 * S], F32, name="y_win%d" % t) for t in range(1, last)]
-        y_win += [keep.tile([P, S], F32, name="y_win3", tag="wb_raw1", align_bytes=64)]
-        y_cpy = [y_win[t + 1][:, S:] for t in range(last - 1)]
-        y_cpy += [keep.tile([P, S], F32, name="y_cpy2")[:]]
+        y_win = [keep.tile([P, S if t == 0 else 2 * S], F32, name="y_win%d" % t) for t in range(PACK)]
+        y_cpy = [y_win[t + 1][:, S:] for t in range(last)]
+        y_cpy.append(keep.tile([P, S], F32, name="y_cpy_last")[:])
+        y_g = keep.tile([P, S], F32, name="y_g")
         for t in range(PACK):
             acc = psum.tile([P, S], F32, name="y_ps%d" % t, tag="ya%d" % t)
             product(acc[:], w1_w, w1_s, t, xq_w, xq_s)
             nc.scalar.copy(y_win[t][:, :S], acc[:])
-            if t < last:
-                nc.sync.dma_start(y_cpy[t], y_win[t][:, :S])
-        y_g = []
-        for i, lst in enumerate((n1_l, n2_l)):
-            g = keep.tile([P, S], F32, name="y_g%d" % i)
-            for h in range(2):
-                nc.scalar.activation(g[:, cols(h)], y_win[last][:].indirect(half_of(lst, h)), COPY)
-            y_g.append(g)
+            nc.sync.dma_start(y_cpy[t], y_win[t][:, :S])
+            if t == 1:
+                for h in range(2):
+                    nc.scalar.activation(y_g[:, cols(h)], y_win[0][:].indirect(half_of(n1_l, h)), COPY)
 
-        cb_w = gather_words_dealt("cb_w", cb_l, "w1_bf")
         cand_g = gather_scales("cand_g", cand_l, "w1_raw1")
         cand_s = deal_scales("cand_s", cand_g)
-        cand_w = gather_words_dealt("cand_w", cand_l, "w1_raw1")
 
+        nc.vector.tensor_copy(*wb_views(1))
         wb_w, wb_s = quantize("wbq", wb_bf[:], S)
+        cand_w = gather_words_dealt("cand_w", cand_l, "w1_raw1")
         b_g, b_win = {}, []
         for t in range(PACK):
             acc = psum.tile([P, S], F32, name="b_ps%d" % t, tag="b%d" % t)
@@ -165,20 +163,20 @@ def tile_picked_cdswclampbquad_none_p_kernel(tc, x_words, x_scales, w1, gs, wb, 
 
         def diff(d, i, t):
             lst = (n1_l, n2_l)[i]
-            if t == 0:
+            if (t, i) == (0, 0):
+                nc.vector.tensor_tensor(d[:, i * S : (i + 1) * S], y_g[:], y_win[t][:], ALU.subtract)
+            elif t == 0:
                 for h in range(2):
                     nc.vector.tensor_tensor(d[:, i * S + h * HALF : i * S + (h + 1) * HALF], y_win[t][:].indirect(half_of(lst, h)), y_cpy[t][:, cols(h)], ALU.subtract)
-            elif t < last:
-                nc.vector.tensor_tensor(d[:, i * S : (i + 1) * S], y_win[t][:].indirect(lst[:]), y_cpy[t], ALU.subtract)
             else:
-                nc.vector.tensor_tensor(d[:, i * S : (i + 1) * S], y_g[i][:], y_win[t][:, :S], ALU.subtract)
+                nc.vector.tensor_tensor(d[:, i * S : (i + 1) * S], y_win[t][:].indirect(lst[:]), y_cpy[t], ALU.subtract)
 
         def z_plane(t, d, lo, hi):
             nc.vector.scalar_tensor_tensor(planes[:, t, lo:hi], d[:, lo:hi], gain[:, t : t + 1], d[:, S + lo : S + hi], ALU.mult, ALU.mult)
 
         prev = None
         for t in range(PACK):
-            d = keep.tile([P, 2 * S], F32, name="d%d" % t, tag=("wb_bf", "w1_bf")[t % 2], align_bytes=64)
+            d = keep.tile([P, 2 * S], F32, name="d%d" % t, tag=("wb_bf", "cb_w")[t % 2], align_bytes=64)
             diff(d, 0, t)
             if prev is not None:
                 z_plane(t - 1, prev, 0, S)
@@ -200,7 +198,7 @@ def tile_picked_cdswclampbquad_none_p_kernel(tc, x_words, x_scales, w1, gs, wb, 
             nc.vector.tensor_copy(g[:, cols(h)], b_win[last][:].indirect(half_of(n5_l, h)))
             b_g[1, last, h] = g[:, cols(h)]
 
-        out_rows = out.rearrange("(p t) n -> p t n", t=PACK)
+        out_rows = out.rearrange("(g t r) n -> t g r n", t=PACK, g=8)
         units = [(t, h * HALF, HALF) for t in range(PACK) for h in range(2)]
         units = units[:-1] + [(last, HALF, HALF // 2), (last, HALF + HALF // 2, HALF // 2)]
 
@@ -210,7 +208,7 @@ def tile_picked_cdswclampbquad_none_p_kernel(tc, x_words, x_scales, w1, gs, wb, 
         def finish(t, lo, n, v):
             o = keep.tile([P, n], F32, name="o%d_%d" % (t, lo))
             nc.vector.tensor_tensor(o[:], v[:, :n], looked_up(1, t, lo, n), ALU.max)
-            nc.sync.dma_start(out_rows[:, t, lo : lo + n], o[:])
+            nc.sync.dma_start(out_rows[t][:, :, lo : lo + n], o[:])
 
         waiting = None
         for t, lo, n in units:

@@ -17,8 +17,15 @@ ALU = mybir.AluOpType
 
 P = 128
 PACK = 4
-HALF = 256
-LIST_COLS = S // 16
+TILES = 4
+LAST = TILES - 1
+GROUP = 16
+GROUPS = P // GROUP
+QUADRANT = 32
+HALF = S // 2
+RUN = 4
+X_FIRST = T // 4
+RING = 3
 
 
 def tile_picked_cdswclampbquad_none_p_kernel(tc, x_words, x_scales, w1, gs, wb, offs, n1, n2, cand, cb, n3, n4, n5, out):
@@ -26,40 +33,40 @@ def tile_picked_cdswclampbquad_none_p_kernel(tc, x_words, x_scales, w1, gs, wb, 
     with ExitStack() as ctx:
         lists = ctx.enter_context(tc.tile_pool(name="lists", bufs=1))
         keep = ctx.enter_context(tc.tile_pool(name="keep", bufs=1))
-        ring = ctx.enter_context(tc.tile_pool(name="ring", bufs=3))
+        ring = ctx.enter_context(tc.tile_pool(name="ring", bufs=RING))
         psum = ctx.enter_context(tc.psum_pool(name="psum", bufs=1))
 
         def load_list(name, src):
-            t = lists.tile([P, LIST_COLS], U16, name=name)
-            nc.sync.dma_start(t[:], src)
-            return t
+            tile = lists.tile([P, S // GROUP], U16, name=name)
+            nc.sync.dma_start(tile[:], src)
+            return tile
 
-        def half_of(lst, h):
-            return lst[:, h * (HALF // 16) : (h + 1) * (HALF // 16)]
+        def entries(lst, lo, n):
+            return lst[:, lo // GROUP : (lo + n) // GROUP]
 
         def cols(h):
             return slice(h * HALF, (h + 1) * HALF)
 
-        xs = keep.tile([P, T], U8, name="xs", align_bytes=64)
-        nc.vector.memset(xs[:].bitcast(I32), 0)
         def load_half(name, w, h):
             raw = keep.tile([P, PACK, HALF], F32, name="%s%d" % (name, h), tag="%s%d" % (name, h), align_bytes=64)
             nc.sync.dma_start(raw[:], w.rearrange("(p j) c -> p j c", j=PACK)[:, :, cols(h)])
             return raw
 
+        xs = keep.tile([P, T], U8, name="xs", align_bytes=64)
+        nc.vector.memset(xs[:].bitcast(I32), 0)
         xw = keep.tile([P, T], U32, name="xw", align_bytes=64)
         x_rows = x_words[0].rearrange("p n t -> p (n t)").bitcast(I32)
         offs_l = load_list("offs_l", offs)
-        nc.sync.dma_start(xw[:, : T // 2].bitcast(I32), x_rows[:, : T // 2])
-        for r in range(4):
-            nc.sync.dma_start(xs[r:P:32, :].bitcast(I32), x_scales[0, r:16:4, :].bitcast(I32))
+        nc.sync.dma_start(xw[:, :X_FIRST].bitcast(I32), x_rows[:, :X_FIRST])
         cb_l = load_list("cb_l", cb)
-        nc.sync.dma_start(xw[:, T // 2 :].bitcast(I32), x_rows[:, T // 2 :])
+        for r in range(4):
+            nc.sync.dma_start(xs[r:P:QUADRANT, :].bitcast(I32), x_scales[0, r:16:4, :].bitcast(I32))
+        nc.sync.dma_start(xw[:, X_FIRST:].bitcast(I32), x_rows[:, X_FIRST:])
         w1_raw = [load_half("w1_raw", w1, h) for h in range(2)]
         cand_l = load_list("cand_l", cand)
         wb_raw = [load_half("wb_raw", wb, h) for h in range(2)]
-        gs_t = keep.tile([P, PACK], F32, name="gs_t")
-        nc.sync.dma_start(gs_t[:], gs.rearrange("(p t) o -> p (t o)", t=PACK))
+        gs_t = keep.tile([P, TILES], F32, name="gs_t")
+        nc.sync.dma_start(gs_t[:], gs.rearrange("(p t) o -> p (t o)", t=TILES))
         n1_l = load_list("n1_l", n1)
         n2_l = load_list("n2_l", n2)
         n4_l = load_list("n4_l", n4)
@@ -67,160 +74,192 @@ def tile_picked_cdswclampbquad_none_p_kernel(tc, x_words, x_scales, w1, gs, wb, 
         n3_l = load_list("n3_l", n3)
 
         def gather_scales(name, lst, tag):
-            g = keep.tile([P, S], U8, name=name, tag=tag, align_bytes=64)
-            nc.vector.tensor_copy(g[:], xs[:].indirect(lst[:]))
-            return g
+            picked = keep.tile([P, S], U8, name=name, tag=tag, align_bytes=64)
+            nc.vector.tensor_copy(picked[:], xs[:].indirect(lst[:]))
+            return picked
 
-        def deal_scales(name, g):
-            d = keep.tile([P, S], U8, name=name, align_bytes=64)
-            nc.vector.tensor_copy(d[:].bitcast(I32).rearrange("p (t g w) -> p t g w", t=PACK, g=8), g[:].bitcast(I32).rearrange("p (g t w) -> p t g w", t=PACK, g=8))
-            return d
+        def deal_scales(name, picked, tag):
+            dealt = keep.tile([P, S], U8, name=name, tag=tag, align_bytes=64)
+            nc.vector.tensor_copy(
+                dealt[:].bitcast(I32).rearrange("p (t g w) -> p t g w", t=TILES, g=GROUPS),
+                picked[:].bitcast(I32).rearrange("p (g t w) -> p t g w", t=TILES, g=GROUPS),
+            )
+            return dealt
 
         def gather_words_dealt(name, lst, tag):
-            d = keep.tile([P, S], U32, name=name, tag=tag, align_bytes=64)
-            nc.vector.tensor_copy(d[:].rearrange("p (t g r) -> p g t r", t=PACK, g=8), xw[:].indirect(lst[:]))
-            return d
+            dealt = keep.tile([P, S], U32, name=name, tag=tag, align_bytes=64)
+            nc.vector.tensor_copy(dealt[:].rearrange("p (t g r) -> p g t r", t=TILES, g=GROUPS), xw[:].indirect(lst[:]))
+            return dealt
 
+        cb_picked = gather_scales("cb_picked", cb_l, "cb_picked")
         xq_s = gather_scales("xq_s", offs_l, "xq_s")
-        cb_g = gather_scales("cb_g", cb_l, "cb_g")
-        cb_s = deal_scales("cb_s", cb_g)
-        xq_w = keep.tile([P, S], U32, name="xq_w", tag="xq_w", align_bytes=64)
+        cb_s = deal_scales("cb_s", cb_picked, "cb_s")
+        xq_w = keep.tile([P, S], U32, name="xq_w", align_bytes=64)
         nc.vector.tensor_copy(xq_w[:], xw[:].indirect(offs_l[:]))
         cb_w = gather_words_dealt("cb_w", cb_l, "cb_w")
 
-        w1_bf = keep.tile([P, H * PACK], BF16, name="w1_bf", tag="w1_bf", align_bytes=64)
+        w1_bf = keep.tile([P, H * PACK], BF16, name="w1_bf", align_bytes=64)
         for h in range(2):
-            m = slice(h * (HALF // PACK), (h + 1) * (HALF // PACK))
+            m = slice(h * (HALF // TILES), (h + 1) * (HALF // TILES))
             nc.scalar.activation(
-                w1_bf[:].rearrange("p (t m j) -> p m t j", t=PACK, j=PACK)[:, m],
-                w1_raw[h][:].rearrange("p j (m t) -> p m t j", t=PACK),
+                w1_bf[:].rearrange("p (t m j) -> p m t j", t=TILES, j=PACK)[:, m],
+                w1_raw[h][:].rearrange("p j (m t) -> p m t j", t=TILES),
                 COPY,
             )
-        gain = keep.tile([P, PACK], F32, name="gain")
-        nc.scalar.activation(gain[:], gs_t[:], COPY, scale=0.75)
 
         def quantize(name, src, width):
-            w = keep.tile([P, width], U32, name=name + "_w", align_bytes=64)
-            s = keep.tile([P, width], U8, name=name + "_s", align_bytes=64)
-            nc.vector.quantize_mx(out=w[:].bitcast(FP8X4), scales=s[:], in_=src)
-            return w, s
+            words = keep.tile([P, width], U32, name=name + "_w", align_bytes=64)
+            scales = keep.tile([P, width], U8, name=name + "_s", align_bytes=64)
+            nc.vector.quantize_mx(out=words[:].bitcast(FP8X4), scales=scales[:], in_=src)
+            return words, scales
 
         w1_w, w1_s = quantize("w1q", w1_bf[:], H)
 
-        def product(acc, lw, ls, t, rw, rs):
+        def product(acc, left_w, left_s, t, right_w, right_s):
             m = slice(t * P, (t + 1) * P)
-            nc.tensor.matmul_mx(out=acc, lhsT=lw[:, m].bitcast(FP8X4), lhsT_scale=ls[:, m],
-                                rhs=rw[:].bitcast(FP8X4), rhs_scale=rs[:], start=True, stop=True)
+            nc.tensor.matmul_mx(
+                out=acc,
+                lhsT=left_w[:, m].bitcast(FP8X4),
+                lhsT_scale=left_s[:, m],
+                rhs=right_w[:].bitcast(FP8X4),
+                rhs_scale=right_s[:],
+                start=True,
+                stop=True,
+            )
 
         wb_bf = keep.tile([P, S * PACK], BF16, name="wb_bf", tag="wb_bf", align_bytes=64)
 
         def wb_views(h):
             return (
-                wb_bf[:, h * HALF * PACK : (h + 1) * HALF * PACK].rearrange("p (c i j) -> p c j i", i=4, j=PACK),
-                wb_raw[h][:].rearrange("p j (c i) -> p c j i", i=4),
+                wb_bf[:, h * HALF * PACK : (h + 1) * HALF * PACK].rearrange("p (c i j) -> p c j i", i=RUN, j=PACK),
+                wb_raw[h][:].rearrange("p j (c i) -> p c j i", i=RUN),
             )
 
         nc.scalar.activation(*wb_views(0), COPY)
 
-        last = PACK - 1
-        y_win = [keep.tile([P, S if t == 0 else 2 * S], F32, name="y_win%d" % t) for t in range(PACK)]
-        y_cpy = [y_win[t + 1][:, S:] for t in range(last)]
-        y_cpy.append(keep.tile([P, S], F32, name="y_cpy_last")[:])
-        y_g = keep.tile([P, S], F32, name="y_g")
-        for t in range(PACK):
+        y_win = [keep.tile([P, S if t in (0, LAST) else 2 * S], F32, name="y_win%d" % t) for t in range(TILES)]
+        y_cpy = [y_win[t + 1][:, S:] for t in range(LAST - 1)]
+        y_cpy = y_cpy + [keep.tile([P, S], F32, name="y_cpy%d" % t)[:] for t in (LAST - 1, LAST)]
+        y_lists = (n1_l, n2_l)
+        y_by_scalar = {}
+
+        def look_up(dst, window, lst, lo, n):
+            nc.scalar.activation(dst, window[:].indirect(entries(lst, lo, n)), COPY)
+
+        def look_up_y(i, t):
+            found = keep.tile([P, S], F32, name="y_found%d" % t)
+            for h in range(2):
+                look_up(found[:, cols(h)], y_win[t], y_lists[i], h * HALF, HALF)
+            y_by_scalar[i, t] = found
+
+        for t in range(TILES):
             acc = psum.tile([P, S], F32, name="y_ps%d" % t, tag="ya%d" % t)
             product(acc[:], w1_w, w1_s, t, xq_w, xq_s)
             nc.scalar.copy(y_win[t][:, :S], acc[:])
             nc.sync.dma_start(y_cpy[t], y_win[t][:, :S])
             if t == 1:
-                for h in range(2):
-                    nc.scalar.activation(y_g[:, cols(h)], y_win[0][:].indirect(half_of(n1_l, h)), COPY)
+                look_up_y(0, 0)
+        gain = keep.tile([P, TILES], F32, name="gain")
+        nc.scalar.activation(gain[:], gs_t[:], COPY, scale=0.75)
+        look_up_y(1, LAST)
 
-        cand_g = gather_scales("cand_g", cand_l, "w1_raw1")
-        cand_s = deal_scales("cand_s", cand_g)
-
+        cand_picked = gather_scales("cand_picked", cand_l, "w1_raw1")
         nc.vector.tensor_copy(*wb_views(1))
+        cand_s = deal_scales("cand_s", cand_picked, "wb_raw1")
         wb_w, wb_s = quantize("wbq", wb_bf[:], S)
         cand_w = gather_words_dealt("cand_w", cand_l, "w1_raw1")
-        b_g, b_win = {}, []
-        for t in range(PACK):
+
+        b_found, b_win = {}, []
+        for t in range(TILES):
             acc = psum.tile([P, S], F32, name="b_ps%d" % t, tag="b%d" % t)
             product(acc[:], cb_w, cb_s, t, wb_w, wb_s)
             win = keep.tile([P, S], F32, name="b_win%d" % t)
             nc.scalar.copy(win[:], acc[:])
             b_win.append(win)
             for i, lst in enumerate((n4_l, n5_l)):
+                found = keep.tile([P, S], F32, name="b_found%d%d" % (i, t))
                 for h in range(2):
-                    if t < last or (i, h) == (0, 0):
-                        g = keep.tile([P, HALF], F32, name="b_g%d%d%d" % (i, t, h))
-                        nc.scalar.activation(g[:], win[:].indirect(half_of(lst, h)), COPY)
-                        b_g[i, t, h] = g[:]
+                    if (i, t, h) != (1, LAST, 1):
+                        look_up(found[:, cols(h)], win, lst, h * HALF, HALF)
+                b_found[i, t] = found
 
-        a_ps = [psum.tile([P, S], F32, name="a_ps%d" % t, tag="ya%d" % t) for t in range(PACK)]
-        a_win = [keep.tile([P, S], F32, name="a_win%d" % t) for t in range(PACK)]
-        planes = keep.tile([P, PACK, S], BF16, name="z_planes", align_bytes=64)
+        a_ps = {t: psum.tile([P, S], F32, name="a_ps%d" % t, tag="ya%d" % t) for t in range(1, TILES)}
+        a_win = [keep.tile([P, S], F32, name="a_win%d" % t) for t in range(TILES)]
+        z_tiles = keep.tile([P, TILES, S], BF16, name="z_tiles", align_bytes=64)
         z_bf = [keep.tile([P, HALF * PACK], BF16, name="z_bf%d" % h, tag="z_bf%d" % h, align_bytes=64) for h in range(2)]
 
-        def diff(d, i, t):
-            lst = (n1_l, n2_l)[i]
-            if (t, i) == (0, 0):
-                nc.vector.tensor_tensor(d[:, i * S : (i + 1) * S], y_g[:], y_win[t][:], ALU.subtract)
-            elif t == 0:
+        def difference(d, i, t):
+            lst = y_lists[i]
+            if (i, t) in y_by_scalar:
+                nc.vector.tensor_tensor(d[:, i * S : (i + 1) * S], y_by_scalar[i, t][:], y_win[t][:], ALU.subtract)
+            elif t in (0, LAST):
                 for h in range(2):
-                    nc.vector.tensor_tensor(d[:, i * S + h * HALF : i * S + (h + 1) * HALF], y_win[t][:].indirect(half_of(lst, h)), y_cpy[t][:, cols(h)], ALU.subtract)
+                    nc.vector.tensor_tensor(
+                        d[:, i * S + h * HALF : i * S + (h + 1) * HALF],
+                        y_win[t][:].indirect(entries(lst, h * HALF, HALF)),
+                        y_cpy[t][:, cols(h)],
+                        ALU.subtract,
+                    )
             else:
                 nc.vector.tensor_tensor(d[:, i * S : (i + 1) * S], y_win[t][:].indirect(lst[:]), y_cpy[t], ALU.subtract)
 
-        def z_plane(t, d, lo, hi):
-            nc.vector.scalar_tensor_tensor(planes[:, t, lo:hi], d[:, lo:hi], gain[:, t : t + 1], d[:, S + lo : S + hi], ALU.mult, ALU.mult)
+        def z_rows(t, d, lo, hi):
+            nc.vector.scalar_tensor_tensor(
+                z_tiles[:, t, lo:hi], d[:, lo:hi], gain[:, t : t + 1], d[:, S + lo : S + hi], ALU.mult, ALU.mult
+            )
 
         prev = None
-        for t in range(PACK):
+        for t in range(TILES):
             d = keep.tile([P, 2 * S], F32, name="d%d" % t, tag=("wb_bf", "cb_w")[t % 2], align_bytes=64)
-            diff(d, 0, t)
-            if prev is not None:
-                z_plane(t - 1, prev, 0, S)
-            diff(d, 1, t)
+            difference(d, 0, t)
+            if 0 < t < LAST:
+                z_rows(t - 1, prev, 0, S)
+            difference(d, 1, t)
+            if t == LAST:
+                z_rows(t - 1, prev, 0, S)
             prev = d
         for h in range(2):
-            z_plane(last, prev, h * HALF, (h + 1) * HALF)
+            z_rows(LAST, prev, h * HALF, (h + 1) * HALF)
         for h in range(2):
-            nc.vector.tensor_copy(z_bf[h][:].rearrange("p (c i t) -> p c t i", i=4, t=PACK), planes[:, :, cols(h)].rearrange("p t (c i) -> p c t i", i=4))
+            nc.vector.tensor_copy(
+                z_bf[h][:].rearrange("p (c i t) -> p c t i", i=RUN, t=PACK),
+                z_tiles[:, :, cols(h)].rearrange("p t (c i) -> p c t i", i=RUN),
+            )
         zq = [quantize("zq%d" % h, z_bf[h][:], HALF) for h in range(2)]
-        for t in range(PACK):
+
+        for h in range(2):
+            acc = psum.tile([P, HALF], F32, name="a_first%d" % h, tag=("ya0", "b0")[h])
+            product(acc[:], cand_w, cand_s, 0, *zq[h])
+            nc.scalar.activation(a_win[0][:, cols(h)], acc[:], COPY, scale=0.0625)
+        for t in range(1, TILES):
             for h in range(2):
                 product(a_ps[t][:, cols(h)], cand_w, cand_s, t, *zq[h])
-        g = keep.tile([P, HALF], F32, name="g4_last", tag="z_bf0", align_bytes=64)
-        nc.vector.tensor_copy(g[:], b_win[last][:].indirect(half_of(n4_l, 1)))
-        b_g[0, last, 1] = g[:]
-        g = keep.tile([P, S], F32, name="g5_last", tag="z_bf1", align_bytes=64)
-        for h in range(2):
-            nc.vector.tensor_copy(g[:, cols(h)], b_win[last][:].indirect(half_of(n5_l, h)))
-            b_g[1, last, h] = g[:, cols(h)]
+        b5_late = keep.tile([P, HALF], F32, name="b5_late", tag="z_bf1", align_bytes=64)
+        nc.vector.tensor_copy(b5_late[:], b_win[LAST][:].indirect(entries(n5_l, HALF, HALF)))
+        nc.vector.tensor_scalar(a_win[1][:], a_ps[1][:], 0.0625, None, ALU.mult)
 
-        out_rows = out.rearrange("(g t r) n -> t g r n", t=PACK, g=8)
-        units = [(t, h * HALF, HALF) for t in range(PACK) for h in range(2)]
-        units = units[:-1] + [(last, HALF, HALF // 2), (last, HALF + HALF // 2, HALF // 2)]
+        out_rows = out.rearrange("(g t r) n -> t g r n", t=TILES, g=GROUPS)
+        pieces = [(0, 0, HALF), (0, HALF, HALF), (1, 0, S), (2, 0, S)]
+        pieces = pieces + [(LAST, 0, HALF), (LAST, HALF, HALF // 2), (LAST, HALF + HALF // 2, HALF // 2)]
 
-        def looked_up(i, t, lo, n):
-            return b_g[i, t, lo // HALF][:, lo % HALF : lo % HALF + n]
-
-        def finish(t, lo, n, v):
-            o = keep.tile([P, n], F32, name="o%d_%d" % (t, lo))
-            nc.vector.tensor_tensor(o[:], v[:, :n], looked_up(1, t, lo, n), ALU.max)
-            nc.sync.dma_start(out_rows[t][:, :, lo : lo + n], o[:])
+        def finish(t, lo, n, low):
+            res = keep.tile([P, n], F32, name="res%d_%d" % (t, lo))
+            b5 = b5_late[:, lo - HALF : lo - HALF + n] if t == LAST and lo >= HALF else b_found[1, t][:, lo : lo + n]
+            nc.vector.tensor_tensor(res[:], low[:, :n], b5, ALU.max)
+            nc.sync.dma_start(out_rows[t][:, :, lo : lo + n], res[:])
 
         waiting = None
-        for t, lo, n in units:
-            if lo == 0:
+        for t, lo, n in pieces:
+            if lo == 0 and t > 1:
                 nc.scalar.activation(a_win[t][:], a_ps[t][:], COPY, scale=0.0625)
-            g3 = ring.tile([P, HALF], F32, name="g3", tag="g3")
-            nc.scalar.activation(g3[:, :n], a_win[t][:].indirect(n3_l[:, lo // 16 : (lo + n) // 16]), COPY)
-            u = ring.tile([P, HALF], F32, name="u", tag="u")
-            nc.vector.scalar_tensor_tensor(u[:, :n], g3[:, :n], -0.5, a_win[t][:, lo : lo + n], ALU.mult, ALU.add)
+            a3 = ring.tile([P, S], F32, name="a3", tag="a3")
+            for at in range(0, n, HALF):
+                look_up(a3[:, at : at + min(n, HALF)], a_win[t], n3_l, lo + at, min(n, HALF))
+            score = ring.tile([P, S], F32, name="score", tag="score")
+            nc.vector.scalar_tensor_tensor(score[:, :n], a3[:, :n], -0.5, a_win[t][:, lo : lo + n], ALU.mult, ALU.add)
             if waiting is not None:
                 finish(*waiting)
-            v = ring.tile([P, HALF], F32, name="v", tag="v")
-            nc.vector.tensor_tensor(v[:, :n], u[:, :n], looked_up(0, t, lo, n), ALU.min)
-            waiting = (t, lo, n, v)
+            low = ring.tile([P, S], F32, name="low", tag="low")
+            nc.vector.tensor_tensor(low[:, :n], score[:, :n], b_found[0, t][:, lo : lo + n], ALU.min)
+            waiting = (t, lo, n, low)
         finish(*waiting)

from contextlib import ExitStack

import concourse.mybir as mybir

K, T, S, H, C = 512, 2048, 512, 512, 512
FLOPS = 2 * K * H * S + 2 * K * C * S + 2 * K * C * S

F32 = mybir.dt.float32
BF16 = mybir.dt.bfloat16
I32 = mybir.dt.int32
U32 = mybir.dt.uint32
U16 = mybir.dt.uint16
U8 = mybir.dt.uint8
FP8X4 = mybir.dt.float8_e4m3fn_x4
COPY = mybir.ActivationFunctionType.Copy
ALU = mybir.AluOpType

P = 128
PACK = 4
TILES = 4
LAST = TILES - 1
GROUP = 16
GROUPS = P // GROUP
QUADRANT = 32
HALF = S // 2
RUN = 4
X_FIRST = T // 4
RING = 3


def tile_picked_cdswclampbquad_none_p_kernel(tc, x_words, x_scales, w1, gs, wb, offs, n1, n2, cand, cb, n3, n4, n5, out):
    nc = tc.nc
    with ExitStack() as ctx:
        lists = ctx.enter_context(tc.tile_pool(name="lists", bufs=1))
        keep = ctx.enter_context(tc.tile_pool(name="keep", bufs=1))
        ring = ctx.enter_context(tc.tile_pool(name="ring", bufs=RING))
        psum = ctx.enter_context(tc.psum_pool(name="psum", bufs=1))

        def load_list(name, src):
            tile = lists.tile([P, S // GROUP], U16, name=name)
            nc.sync.dma_start(tile[:], src)
            return tile

        def entries(lst, lo, n):
            return lst[:, lo // GROUP : (lo + n) // GROUP]

        def cols(h):
            return slice(h * HALF, (h + 1) * HALF)

        def load_half(name, w, h):
            raw = keep.tile([P, PACK, HALF], F32, name="%s%d" % (name, h), tag="%s%d" % (name, h), align_bytes=64)
            nc.sync.dma_start(raw[:], w.rearrange("(p j) c -> p j c", j=PACK)[:, :, cols(h)])
            return raw

        xs = keep.tile([P, T], U8, name="xs", align_bytes=64)
        nc.vector.memset(xs[:].bitcast(I32), 0)
        xw = keep.tile([P, T], U32, name="xw", align_bytes=64)
        x_rows = x_words[0].rearrange("p n t -> p (n t)").bitcast(I32)
        offs_l = load_list("offs_l", offs)
        nc.sync.dma_start(xw[:, :X_FIRST].bitcast(I32), x_rows[:, :X_FIRST])
        cb_l = load_list("cb_l", cb)
        for r in range(4):
            nc.sync.dma_start(xs[r:P:QUADRANT, :].bitcast(I32), x_scales[0, r:16:4, :].bitcast(I32))
        nc.sync.dma_start(xw[:, X_FIRST:].bitcast(I32), x_rows[:, X_FIRST:])
        w1_raw = [load_half("w1_raw", w1, h) for h in range(2)]
        cand_l = load_list("cand_l", cand)
        wb_raw = [load_half("wb_raw", wb, h) for h in range(2)]
        gs_t = keep.tile([P, TILES], F32, name="gs_t")
        nc.sync.dma_start(gs_t[:], gs.rearrange("(p t) o -> p (t o)", t=TILES))
        n1_l = load_list("n1_l", n1)
        n2_l = load_list("n2_l", n2)
        n4_l = load_list("n4_l", n4)
        n5_l = load_list("n5_l", n5)
        n3_l = load_list("n3_l", n3)

        def gather_scales(name, lst, tag):
            picked = keep.tile([P, S], U8, name=name, tag=tag, align_bytes=64)
            nc.vector.tensor_copy(picked[:], xs[:].indirect(lst[:]))
            return picked

        def deal_scales(name, picked, tag):
            dealt = keep.tile([P, S], U8, name=name, tag=tag, align_bytes=64)
            nc.vector.tensor_copy(
                dealt[:].bitcast(I32).rearrange("p (t g w) -> p t g w", t=TILES, g=GROUPS),
                picked[:].bitcast(I32).rearrange("p (g t w) -> p t g w", t=TILES, g=GROUPS),
            )
            return dealt

        def gather_words_dealt(name, lst, tag):
            dealt = keep.tile([P, S], U32, name=name, tag=tag, align_bytes=64)
            nc.vector.tensor_copy(dealt[:].rearrange("p (t g r) -> p g t r", t=TILES, g=GROUPS), xw[:].indirect(lst[:]))
            return dealt

        cb_picked = gather_scales("cb_picked", cb_l, "cb_picked")
        xq_s = gather_scales("xq_s", offs_l, "xq_s")
        cb_s = deal_scales("cb_s", cb_picked, "cb_s")
        xq_w = keep.tile([P, S], U32, name="xq_w", align_bytes=64)
        nc.vector.tensor_copy(xq_w[:], xw[:].indirect(offs_l[:]))
        cb_w = gather_words_dealt("cb_w", cb_l, "cb_w")

        w1_bf = keep.tile([P, H * PACK], BF16, name="w1_bf", align_bytes=64)
        for h in range(2):
            m = slice(h * (HALF // TILES), (h + 1) * (HALF // TILES))
            nc.scalar.activation(
                w1_bf[:].rearrange("p (t m j) -> p m t j", t=TILES, j=PACK)[:, m],
                w1_raw[h][:].rearrange("p j (m t) -> p m t j", t=TILES),
                COPY,
            )

        def quantize(name, src, width):
            words = keep.tile([P, width], U32, name=name + "_w", align_bytes=64)
            scales = keep.tile([P, width], U8, name=name + "_s", align_bytes=64)
            nc.vector.quantize_mx(out=words[:].bitcast(FP8X4), scales=scales[:], in_=src)
            return words, scales

        w1_w, w1_s = quantize("w1q", w1_bf[:], H)

        def product(acc, left_w, left_s, t, right_w, right_s):
            m = slice(t * P, (t + 1) * P)
            nc.tensor.matmul_mx(
                out=acc,
                lhsT=left_w[:, m].bitcast(FP8X4),
                lhsT_scale=left_s[:, m],
                rhs=right_w[:].bitcast(FP8X4),
                rhs_scale=right_s[:],
                start=True,
                stop=True,
            )

        wb_bf = keep.tile([P, S * PACK], BF16, name="wb_bf", tag="wb_bf", align_bytes=64)

        def wb_views(h):
            return (
                wb_bf[:, h * HALF * PACK : (h + 1) * HALF * PACK].rearrange("p (c i j) -> p c j i", i=RUN, j=PACK),
                wb_raw[h][:].rearrange("p j (c i) -> p c j i", i=RUN),
            )

        nc.scalar.activation(*wb_views(0), COPY)

        y_win = [keep.tile([P, S if t in (0, LAST) else 2 * S], F32, name="y_win%d" % t) for t in range(TILES)]
        y_cpy = [y_win[t + 1][:, S:] for t in range(LAST - 1)]
        y_cpy = y_cpy + [keep.tile([P, S], F32, name="y_cpy%d" % t)[:] for t in (LAST - 1, LAST)]
        y_lists = (n1_l, n2_l)
        y_by_scalar = {}

        def look_up(dst, window, lst, lo, n):
            nc.scalar.activation(dst, window[:].indirect(entries(lst, lo, n)), COPY)

        def look_up_y(i, t):
            found = keep.tile([P, S], F32, name="y_found%d" % t)
            for h in range(2):
                look_up(found[:, cols(h)], y_win[t], y_lists[i], h * HALF, HALF)
            y_by_scalar[i, t] = found

        for t in range(TILES):
            acc = psum.tile([P, S], F32, name="y_ps%d" % t, tag="ya%d" % t)
            product(acc[:], w1_w, w1_s, t, xq_w, xq_s)
            nc.scalar.copy(y_win[t][:, :S], acc[:])
            nc.sync.dma_start(y_cpy[t], y_win[t][:, :S])
            if t == 1:
                look_up_y(0, 0)
        gain = keep.tile([P, TILES], F32, name="gain")
        nc.scalar.activation(gain[:], gs_t[:], COPY, scale=0.75)
        look_up_y(1, LAST)

        cand_picked = gather_scales("cand_picked", cand_l, "w1_raw1")
        nc.vector.tensor_copy(*wb_views(1))
        cand_s = deal_scales("cand_s", cand_picked, "wb_raw1")
        wb_w, wb_s = quantize("wbq", wb_bf[:], S)
        cand_w = gather_words_dealt("cand_w", cand_l, "w1_raw1")

        b_found, b_win = {}, []
        for t in range(TILES):
            acc = psum.tile([P, S], F32, name="b_ps%d" % t, tag="b%d" % t)
            product(acc[:], cb_w, cb_s, t, wb_w, wb_s)
            win = keep.tile([P, S], F32, name="b_win%d" % t)
            nc.scalar.copy(win[:], acc[:])
            b_win.append(win)
            for i, lst in enumerate((n4_l, n5_l)):
                found = keep.tile([P, S], F32, name="b_found%d%d" % (i, t))
                for h in range(2):
                    if (i, t, h) != (1, LAST, 1):
                        look_up(found[:, cols(h)], win, lst, h * HALF, HALF)
                b_found[i, t] = found

        a_ps = {t: psum.tile([P, S], F32, name="a_ps%d" % t, tag="ya%d" % t) for t in range(1, TILES)}
        a_win = [keep.tile([P, S], F32, name="a_win%d" % t) for t in range(TILES)]
        z_tiles = keep.tile([P, TILES, S], BF16, name="z_tiles", align_bytes=64)
        z_bf = [keep.tile([P, HALF * PACK], BF16, name="z_bf%d" % h, tag="z_bf%d" % h, align_bytes=64) for h in range(2)]

        def difference(d, i, t):
            lst = y_lists[i]
            if (i, t) in y_by_scalar:
                nc.vector.tensor_tensor(d[:, i * S : (i + 1) * S], y_by_scalar[i, t][:], y_win[t][:], ALU.subtract)
            elif t in (0, LAST):
                for h in range(2):
                    nc.vector.tensor_tensor(
                        d[:, i * S + h * HALF : i * S + (h + 1) * HALF],
                        y_win[t][:].indirect(entries(lst, h * HALF, HALF)),
                        y_cpy[t][:, cols(h)],
                        ALU.subtract,
                    )
            else:
                nc.vector.tensor_tensor(d[:, i * S : (i + 1) * S], y_win[t][:].indirect(lst[:]), y_cpy[t], ALU.subtract)

        def z_rows(t, d, lo, hi):
            nc.vector.scalar_tensor_tensor(
                z_tiles[:, t, lo:hi], d[:, lo:hi], gain[:, t : t + 1], d[:, S + lo : S + hi], ALU.mult, ALU.mult
            )

        prev = None
        for t in range(TILES):
            d = keep.tile([P, 2 * S], F32, name="d%d" % t, tag=("wb_bf", "cb_w")[t % 2], align_bytes=64)
            difference(d, 0, t)
            if 0 < t < LAST:
                z_rows(t - 1, prev, 0, S)
            difference(d, 1, t)
            if t == LAST:
                z_rows(t - 1, prev, 0, S)
            prev = d
        for h in range(2):
            z_rows(LAST, prev, h * HALF, (h + 1) * HALF)
        for h in range(2):
            nc.vector.tensor_copy(
                z_bf[h][:].rearrange("p (c i t) -> p c t i", i=RUN, t=PACK),
                z_tiles[:, :, cols(h)].rearrange("p t (c i) -> p c t i", i=RUN),
            )
        zq = [quantize("zq%d" % h, z_bf[h][:], HALF) for h in range(2)]

        for h in range(2):
            acc = psum.tile([P, HALF], F32, name="a_first%d" % h, tag=("ya0", "b0")[h])
            product(acc[:], cand_w, cand_s, 0, *zq[h])
            nc.scalar.activation(a_win[0][:, cols(h)], acc[:], COPY, scale=0.0625)
        for t in range(1, TILES):
            for h in range(2):
                product(a_ps[t][:, cols(h)], cand_w, cand_s, t, *zq[h])
        b5_late = keep.tile([P, HALF], F32, name="b5_late", tag="z_bf1", align_bytes=64)
        nc.vector.tensor_copy(b5_late[:], b_win[LAST][:].indirect(entries(n5_l, HALF, HALF)))
        nc.vector.tensor_scalar(a_win[1][:], a_ps[1][:], 0.0625, None, ALU.mult)

        out_rows = out.rearrange("(g t r) n -> t g r n", t=TILES, g=GROUPS)
        pieces = [(0, 0, HALF), (0, HALF, HALF), (1, 0, S), (2, 0, S)]
        pieces = pieces + [(LAST, 0, HALF), (LAST, HALF, HALF // 2), (LAST, HALF + HALF // 2, HALF // 2)]

        def finish(t, lo, n, low):
            res = keep.tile([P, n], F32, name="res%d_%d" % (t, lo))
            b5 = b5_late[:, lo - HALF : lo - HALF + n] if t == LAST and lo >= HALF else b_found[1, t][:, lo : lo + n]
            nc.vector.tensor_tensor(res[:], low[:, :n], b5, ALU.max)
            nc.sync.dma_start(out_rows[t][:, :, lo : lo + n], res[:])

        waiting = None
        for t, lo, n in pieces:
            if lo == 0 and t > 1:
                nc.scalar.activation(a_win[t][:], a_ps[t][:], COPY, scale=0.0625)
            a3 = ring.tile([P, S], F32, name="a3", tag="a3")
            for at in range(0, n, HALF):
                look_up(a3[:, at : at + min(n, HALF)], a_win[t], n3_l, lo + at, min(n, HALF))
            score = ring.tile([P, S], F32, name="score", tag="score")
            nc.vector.scalar_tensor_tensor(score[:, :n], a3[:, :n], -0.5, a_win[t][:, lo : lo + n], ALU.mult, ALU.add)
            if waiting is not None:
                finish(*waiting)
            low = ring.tile([P, S], F32, name="low", tag="low")
            nc.vector.tensor_tensor(low[:, :n], score[:, :n], b_found[0, t][:, lo : lo + n], ALU.min)
            waiting = (t, lo, n, low)
        finish(*waiting)
